import numpy as np
import ml_dtypes


def mxq(x, axis, fmt="e4m3"):
    dtype, down = {"e4m3": (ml_dtypes.float8_e4m3fn, 7), "e5m2": (ml_dtypes.float8_e5m2, 14)}[fmt]
    v = np.moveaxis(np.asarray(x, np.float32).astype(ml_dtypes.bfloat16).astype(np.float64), axis, -1)
    blocks = v.reshape(v.shape[:-1] + (-1, 32))
    amax = np.abs(blocks).max(-1, keepdims=True)
    byte = np.maximum(np.where(amax > 0, np.frexp(amax)[1] - 1 + 127, 0) - down, 1)
    scale = np.exp2(byte - 127.0)
    codes = (blocks / scale).astype(np.float32).astype(dtype).astype(np.float64)
    return np.moveaxis((codes * scale).reshape(v.shape), -1, axis)


WIDE = False


def mx_kscale(k):
    if not WIDE:
        return np.ones(k)
    levels = np.array([10, -10, 5, -5, 0])
    if k % 512:
        return np.exp2(np.random.permutation(np.resize(levels, k // 32))).repeat(32)
    a = np.empty((k // 512, 16))
    for p in range(k // 512):
        a[p, :8] = np.random.permutation(np.resize(levels, 8))
        for g in range(8):
            far = levels[np.abs(levels - a[p, g]) >= 10]
            a[p, g + 8] = far[np.random.randint(len(far))]
    return np.exp2(a.ravel()).repeat(32)


def f64(x):
    return np.asarray(x).astype(np.float64)


def striped(idx):
    return np.tile(idx.reshape(-1, 16).T, (8, 1)).astype(np.uint16)


def unstriped(offs):
    return offs[:16].T.reshape(-1).astype(np.int64)


K, T, E, C, N = 512, 1024, 4, 256, 128


def by_expert(wq, xq):
    return np.concatenate([wq[e].T @ xq[:, e * C:(e + 1) * C] for e in range(E)], axis=1)


def setup_inputs():
    n = np.random.standard_normal
    s = mx_kscale(K)[:, None]
    return {
        "xT": (n((K, T)) * s).astype(np.float32),
        "w": (n((E, K, N)) / np.sqrt(K) / s[None]).astype(np.float32),
        "gate": np.tile(np.random.uniform(0.2, 1.0, E * C), (N, 1)).astype(np.float32),
        "offs": striped(np.random.permutation(T)[:E * C]),
    }


def reference(xT, w, gate, offs):
    idx = unstriped(offs)
    xq = mxq(f64(xT)[:, idx], 0, "e4m3")
    y = by_expert(mxq(f64(w), 1, "e4m3"), xq)
    out = np.zeros((N, T))
    out[:, idx] = f64(gate) * y
    return out

@@ -1,0 +1,170 @@
+from contextlib import ExitStack
+
+import concourse.mybir as mybir
+
+K, T, E, C, N = 512, 1024, 4, 256, 128
+FLOPS = 2 * K * N * E * C
+
+F32 = mybir.dt.float32
+BF16 = mybir.dt.bfloat16
+U32 = mybir.dt.uint32
+U16 = mybir.dt.uint16
+U8 = mybir.dt.uint8
+FP8X4 = mybir.dt.float8_e4m3fn_x4
+MULT = mybir.AluOpType.mult
+COPY = mybir.ActivationFunctionType.Copy
+
+P = 128
+PACK = 4
+H = C // 2
+
+
+def tile_routed_moe_kernel(tc, xT, w, gate, offs, out):
+    nc = tc.nc
+    with ExitStack() as ctx:
+        keep = ctx.enter_context(tc.tile_pool(name="keep", bufs=1))
+        psum = ctx.enter_context(tc.psum_pool(name="psum", bufs=1))
+
+        warm_in = keep.tile([P, 1], F32, name="warm_in")
+        warm_out = keep.tile([P, 1], F32, name="warm_out")
+        nc.gpsimd.memset(warm_in[:], 0.0)
+        nc.scalar.activation(warm_out[:], warm_in[:], COPY)
+
+        offsets = keep.tile([P, E * C // 16], U16, name="offsets")
+        nc.sync.dma_start(offsets[:], offs)
+
+        def offs_of(first, n):
+            return offsets[:, first // 16 : (first + n) // 16]
+
+        x_view = xT.rearrange("(p t) n -> p t n", t=PACK)
+        w_view = w.rearrange("e (p j) n -> p e j n", j=PACK)
+        planes = [keep.tile([P, T], F32, name="x_plane%d" % t) for t in range(PACK)]
+        planes_bf = [keep.tile([P, T], BF16, name="x_bf%d" % t) for t in range(PACK)]
+        w_raw01 = keep.tile([P, 2, PACK, N], F32, name="w_raw01")
+        w_raw2 = keep.tile([P, PACK, N], F32, name="w_raw2")
+        w_raw3 = keep.tile([P, PACK, N], F32, name="w_raw3", tag="after_w3", align_bytes=64)
+        w_rows = [w_raw01[:, 0, :, :], w_raw01[:, 1, :, :], w_raw2[:], w_raw3[:]]
+        gate_sb = keep.tile([P, E * C], F32, name="gate_rows")
+        for t in range(PACK):
+            nc.sync.dma_start(planes[t][:], x_view[:, t, :])
+        nc.sync.dma_start(w_raw01[:], w_view[:, 0:2, :, :])
+        nc.sync.dma_start(w_raw2[:], w_view[:, 2, :, :])
+        nc.sync.dma_start(w_raw3[:], w_view[:, 3, :, :])
+        nc.sync.dma_start(gate_sb[:], gate)
+
+        window = keep.tile([P, T], F32, name="window")
+
+        def interleave_weights(engine_copies, i, w_grouped):
+            for h, engine_copy in enumerate(engine_copies):
+                engine_copy(
+                    w_grouped[:, h, :, :].rearrange("p (c i) j -> p c j i", i=4),
+                    w_rows[2 * i + h].rearrange("p j (c i) -> p c j i", i=4),
+                )
+
+        def quantize(codes, scales, grouped):
+            nc.vector.quantize_mx(out=codes.bitcast(FP8X4), scales=scales, in_=grouped)
+
+        def multiply(name, n, w_codes, w_scales, h, codes, scales):
+            acc = psum.tile([P, n], F32, name=name)
+            nc.tensor.matmul_mx(
+                out=acc[:],
+                lhsT=w_codes[:, h * N : (h + 1) * N].bitcast(FP8X4),
+                lhsT_scale=w_scales[:, h * N : (h + 1) * N],
+                rhs=codes.bitcast(FP8X4),
+                rhs_scale=scales,
+                start=True,
+                stop=True,
+            )
+            return acc
+
+        def scalar_gather(grouped, t, first, n):
+            nc.scalar.activation(
+                grouped.rearrange("p (s t) -> p s t", t=PACK)[:, :, t],
+                planes_bf[t][:].indirect(offs_of(first, n)),
+                COPY,
+            )
+
+        def put_back(sums, first, n):
+            nc.vector.tensor_tensor(window[:].indirect(offs_of(first, n)), sums, gate_sb[:, first : first + n], MULT)
+
+        g4 = keep.tile([P, PACK, C], F32, name="g4")
+        grouped1 = keep.tile([P, C * PACK], BF16, name="grouped1", tag="after_q1", align_bytes=64)
+        grouped3a = keep.tile([P, H * PACK], BF16, name="grouped3a", align_bytes=64)
+        for t in range(PACK):
+            (nc.vector).tensor_copy(planes_bf[t][:], planes[t][:])
+            nc.vector.tensor_copy(g4[:, t, :], planes[t][:].indirect(offs_of(0, C)))
+            scalar_gather(grouped1[:], t, C, C)
+            scalar_gather(grouped3a[:], t, 3 * C, H)
+
+        grouped0 = keep.tile([P, C * PACK], BF16, name="grouped0", align_bytes=64)
+        nc.vector.tensor_copy(
+            grouped0[:].rearrange("p (c i t) -> p c t i", i=4, t=PACK),
+            g4[:].rearrange("p t (c i) -> p c t i", i=4),
+        )
+        w_grouped0 = keep.tile([P, 1, N, PACK], BF16, name="w_grouped0", align_bytes=64)
+        w_codes0 = keep.tile([P, N], U32, name="w_codes0", align_bytes=64)
+        w_scales0 = keep.tile([P, N], U8, name="w_scales0", align_bytes=64)
+        interleave_weights((nc.vector.tensor_copy,), 0, w_grouped0)
+        quantize(w_codes0[:], w_scales0[:], w_grouped0[:].rearrange("p e n j -> p (e n j)"))
+
+        codes0 = keep.tile([P, C], U32, name="codes0", align_bytes=64)
+        scales0 = keep.tile([P, C], U8, name="scales0", align_bytes=64)
+        quantize(codes0[:], scales0[:], grouped0[:])
+        acc0 = multiply("acc0", C, w_codes0, w_scales0, 0, codes0[:], scales0[:])
+        w_grouped1 = keep.tile([P, 1, N, PACK], BF16, name="w_grouped1", tag="after_qw01", align_bytes=64)
+        w_codes1 = keep.tile([P, N], U32, name="w_codes1", align_bytes=64)
+        w_scales1 = keep.tile([P, N], U8, name="w_scales1", align_bytes=64)
+        nc.vector.tensor_copy(
+            w_grouped1[:, 0, :, :].rearrange("p (c i) j -> p c j i", i=4),
+            w_rows[1].rearrange("p j (c i) -> p c j i", i=4),
+        )
+        quantize(w_codes1[:], w_scales1[:], w_grouped1[:].rearrange("p e n j -> p (e n j)"))
+        codes1 = keep.tile([P, C], U32, name="codes1", tag="after_qw01", align_bytes=64)
+        scales1 = keep.tile([P, C], U8, name="scales1", align_bytes=64)
+        quantize(codes1[:], scales1[:], grouped1[:])
+        acc1 = multiply("acc1", C, w_codes1, w_scales1, 0, codes1[:], scales1[:])
+        codes3a = keep.tile([P, H], U32, name="codes3a", tag="after_q1", align_bytes=64)
+        scales3a = keep.tile([P, H], U8, name="scales3a", align_bytes=64)
+        quantize(codes3a[:], scales3a[:], grouped3a[:])
+
+        w_grouped23 = keep.tile([P, 2, N, PACK], BF16, name="w_grouped23", align_bytes=64)
+        interleave_weights((nc.vector.tensor_copy, nc.scalar.copy), 1, w_grouped23)
+        late = keep.tile([P, (C + H) * PACK], BF16, name="grouped_late", tag="after_w3", align_bytes=64)
+        grouped2 = late[:, 0 : C * PACK]
+        grouped3b = late[:, C * PACK : (C + H) * PACK]
+        sums0 = keep.tile([P, C], F32, name="sums0", tag="after_sc0", align_bytes=64)
+        nc.vector.tensor_copy(sums0[:], acc0[:])
+        scalar_gather(grouped2, 0, 2 * C, C)
+        sums1 = keep.tile([P, C], F32, name="sums1", tag="after_sc1", align_bytes=64)
+        nc.scalar.copy(sums1[:], acc1[:])
+        for t in range(1, PACK):
+            scalar_gather(grouped2, t, 2 * C, C)
+
+        w_codes23 = keep.tile([P, 2 * N], U32, name="w_codes23", align_bytes=64)
+        w_scales23 = keep.tile([P, 2 * N], U8, name="w_scales23", align_bytes=64)
+        quantize(w_codes23[:], w_scales23[:], w_grouped23[:].rearrange("p e n j -> p (e n j)"))
+        acc3a = multiply("acc3a", H, w_codes23, w_scales23, 1, codes3a[:], scales3a[:])
+        put_back(sums0[:], 0, C)
+        sums3a = keep.tile([P, H], F32, name="sums3a")
+        nc.scalar.copy(sums3a[:], acc3a[:])
+        for t in range(PACK):
+            scalar_gather(grouped3b, t, 3 * C + H, H)
+        put_back(sums1[:], C, C)
+
+        codes2 = keep.tile([P, C], U32, name="codes2", tag="after_sc0", align_bytes=64)
+        scales2 = keep.tile([P, C], U8, name="scales2", align_bytes=64)
+        quantize(codes2[:], scales2[:], grouped2)
+        acc2 = multiply("acc2", C, w_codes23, w_scales23, 0, codes2[:], scales2[:])
+        put_back(sums3a[:], 3 * C, H)
+        codes3b = keep.tile([P, H], U32, name="codes3b", tag="after_sc1", align_bytes=64)
+        scales3b = keep.tile([P, H], U8, name="scales3b", align_bytes=64)
+        quantize(codes3b[:], scales3b[:], grouped3b)
+        acc3b = multiply("acc3b", H, w_codes23, w_scales23, 1, codes3b[:], scales3b[:])
+        sums2 = keep.tile([P, C], F32, name="sums2")
+        nc.scalar.copy(sums2[:], acc2[:])
+        put_back(sums2[:], 2 * C, C)
+        sums3b = keep.tile([P, H], F32, name="sums3b")
+        nc.scalar.copy(sums3b[:], acc3b[:])
+        put_back(sums3b[:], 3 * C + H, H)
+
+        nc.sync.dma_start(out, window[:])

@@ -91,8 +91,13 @@ def tile_routed_moe_kernel(tc, xT, w, gate, offs, out):
         grouped1 = keep.tile([P, C * PACK], BF16, name="grouped1", tag="after_q1", align_bytes=64)
         grouped3a = keep.tile([P, H * PACK], BF16, name="grouped3a", align_bytes=64)
         for t in range(PACK):
-            (nc.vector).tensor_copy(planes_bf[t][:], planes[t][:])
+            if t < 2:
+                nc.vector.tensor_copy(planes_bf[t][:], planes[t][:])
+            elif t == 2:
+                nc.gpsimd.tensor_copy(planes_bf[t][:], planes[t][:])
             nc.vector.tensor_copy(g4[:, t, :], planes[t][:].indirect(offs_of(0, C)))
+            if t == 3:
+                nc.vector.tensor_copy(planes_bf[t][:], planes[t][:])
             scalar_gather(grouped1[:], t, C, C)
             scalar_gather(grouped3a[:], t, 3 * C, H)
 

@@ -17,6 +17,7 @@ COPY = mybir.ActivationFunctionType.Copy
 P = 128
 PACK = 4
 H = C // 2
+HALVES = (slice(0, T // 2), slice(T // 2, T))
 
 
 def tile_routed_moe_kernel(tc, xT, w, gate, offs, out):
@@ -45,8 +46,12 @@ def tile_routed_moe_kernel(tc, xT, w, gate, offs, out):
         w_raw3 = keep.tile([P, PACK, N], F32, name="w_raw3", tag="after_w3", align_bytes=64)
         w_rows = [w_raw01[:, 0, :, :], w_raw01[:, 1, :, :], w_raw2[:], w_raw3[:]]
         gate_sb = keep.tile([P, E * C], F32, name="gate_rows")
-        for t in range(PACK):
-            nc.sync.dma_start(planes[t][:], x_view[:, t, :])
+        for half in HALVES:
+            nc.sync.dma_start(planes[0][:, half], x_view[:, 0, half])
+        nc.sync.dma_start(planes[1][:], x_view[:, 1, :])
+        for half in HALVES:
+            nc.sync.dma_start(planes[2][:, half], x_view[:, 2, half])
+        nc.sync.dma_start(planes[3][:], x_view[:, 3, :])
         nc.sync.dma_start(w_raw01[:], w_view[:, 0:2, :, :])
         nc.sync.dma_start(w_raw2[:], w_view[:, 2, :, :])
         nc.sync.dma_start(w_raw3[:], w_view[:, 3, :, :])
@@ -91,10 +96,14 @@ def tile_routed_moe_kernel(tc, xT, w, gate, offs, out):
         grouped1 = keep.tile([P, C * PACK], BF16, name="grouped1", tag="after_q1", align_bytes=64)
         grouped3a = keep.tile([P, H * PACK], BF16, name="grouped3a", align_bytes=64)
         for t in range(PACK):
-            if t < 2:
+            if t == 0:
+                for half in HALVES:
+                    nc.vector.tensor_copy(planes_bf[t][:, half], planes[t][:, half])
+            elif t == 1:
                 nc.vector.tensor_copy(planes_bf[t][:], planes[t][:])
             elif t == 2:
-                nc.gpsimd.tensor_copy(planes_bf[t][:], planes[t][:])
+                for half in HALVES:
+                    nc.gpsimd.tensor_copy(planes_bf[t][:, half], planes[t][:, half])
             nc.vector.tensor_copy(g4[:, t, :], planes[t][:].indirect(offs_of(0, C)))
             if t == 3:
                 nc.vector.tensor_copy(planes_bf[t][:], planes[t][:])

from contextlib import ExitStack

import concourse.mybir as mybir

K, T, E, C, N = 512, 1024, 4, 256, 128
FLOPS = 2 * K * N * E * C

F32 = mybir.dt.float32
BF16 = mybir.dt.bfloat16
U32 = mybir.dt.uint32
U16 = mybir.dt.uint16
U8 = mybir.dt.uint8
FP8X4 = mybir.dt.float8_e4m3fn_x4
MULT = mybir.AluOpType.mult
COPY = mybir.ActivationFunctionType.Copy

P = 128
PACK = 4
H = C // 2
HALVES = (slice(0, T // 2), slice(T // 2, T))


def tile_routed_moe_kernel(tc, xT, w, gate, offs, out):
    nc = tc.nc
    with ExitStack() as ctx:
        keep = ctx.enter_context(tc.tile_pool(name="keep", bufs=1))
        psum = ctx.enter_context(tc.psum_pool(name="psum", bufs=1))

        warm_in = keep.tile([P, 1], F32, name="warm_in")
        warm_out = keep.tile([P, 1], F32, name="warm_out")
        nc.gpsimd.memset(warm_in[:], 0.0)
        nc.scalar.activation(warm_out[:], warm_in[:], COPY)

        offsets = keep.tile([P, E * C // 16], U16, name="offsets")
        nc.sync.dma_start(offsets[:], offs)

        def offs_of(first, n):
            return offsets[:, first // 16 : (first + n) // 16]

        x_view = xT.rearrange("(p t) n -> p t n", t=PACK)
        w_view = w.rearrange("e (p j) n -> p e j n", j=PACK)
        planes = [keep.tile([P, T], F32, name="x_plane%d" % t) for t in range(PACK)]
        planes_bf = [keep.tile([P, T], BF16, name="x_bf%d" % t) for t in range(PACK)]
        w_raw01 = keep.tile([P, 2, PACK, N], F32, name="w_raw01")
        w_raw2 = keep.tile([P, PACK, N], F32, name="w_raw2")
        w_raw3 = keep.tile([P, PACK, N], F32, name="w_raw3", tag="after_w3", align_bytes=64)
        w_rows = [w_raw01[:, 0, :, :], w_raw01[:, 1, :, :], w_raw2[:], w_raw3[:]]
        gate_sb = keep.tile([P, E * C], F32, name="gate_rows")
        for half in HALVES:
            nc.sync.dma_start(planes[0][:, half], x_view[:, 0, half])
        nc.sync.dma_start(planes[1][:], x_view[:, 1, :])
        for half in HALVES:
            nc.sync.dma_start(planes[2][:, half], x_view[:, 2, half])
        nc.sync.dma_start(planes[3][:], x_view[:, 3, :])
        nc.sync.dma_start(w_raw01[:], w_view[:, 0:2, :, :])
        nc.sync.dma_start(w_raw2[:], w_view[:, 2, :, :])
        nc.sync.dma_start(w_raw3[:], w_view[:, 3, :, :])
        nc.sync.dma_start(gate_sb[:], gate)

        window = keep.tile([P, T], F32, name="window")

        def interleave_weights(engine_copies, i, w_grouped):
            for h, engine_copy in enumerate(engine_copies):
                engine_copy(
                    w_grouped[:, h, :, :].rearrange("p (c i) j -> p c j i", i=4),
                    w_rows[2 * i + h].rearrange("p j (c i) -> p c j i", i=4),
                )

        def quantize(codes, scales, grouped):
            nc.vector.quantize_mx(out=codes.bitcast(FP8X4), scales=scales, in_=grouped)

        def multiply(name, n, w_codes, w_scales, h, codes, scales):
            acc = psum.tile([P, n], F32, name=name)
            nc.tensor.matmul_mx(
                out=acc[:],
                lhsT=w_codes[:, h * N : (h + 1) * N].bitcast(FP8X4),
                lhsT_scale=w_scales[:, h * N : (h + 1) * N],
                rhs=codes.bitcast(FP8X4),
                rhs_scale=scales,
                start=True,
                stop=True,
            )
            return acc

        def scalar_gather(grouped, t, first, n):
            nc.scalar.activation(
                grouped.rearrange("p (s t) -> p s t", t=PACK)[:, :, t],
                planes_bf[t][:].indirect(offs_of(first, n)),
                COPY,
            )

        def put_back(sums, first, n):
            nc.vector.tensor_tensor(window[:].indirect(offs_of(first, n)), sums, gate_sb[:, first : first + n], MULT)

        g4 = keep.tile([P, PACK, C], F32, name="g4")
        grouped1 = keep.tile([P, C * PACK], BF16, name="grouped1", tag="after_q1", align_bytes=64)
        grouped3a = keep.tile([P, H * PACK], BF16, name="grouped3a", align_bytes=64)
        for t in range(PACK):
            if t == 0:
                for half in HALVES:
                    nc.vector.tensor_copy(planes_bf[t][:, half], planes[t][:, half])
            elif t == 1:
                nc.vector.tensor_copy(planes_bf[t][:], planes[t][:])
            elif t == 2:
                for half in HALVES:
                    nc.gpsimd.tensor_copy(planes_bf[t][:, half], planes[t][:, half])
            nc.vector.tensor_copy(g4[:, t, :], planes[t][:].indirect(offs_of(0, C)))
            if t == 3:
                nc.vector.tensor_copy(planes_bf[t][:], planes[t][:])
            scalar_gather(grouped1[:], t, C, C)
            scalar_gather(grouped3a[:], t, 3 * C, H)

        grouped0 = keep.tile([P, C * PACK], BF16, name="grouped0", align_bytes=64)
        nc.vector.tensor_copy(
            grouped0[:].rearrange("p (c i t) -> p c t i", i=4, t=PACK),
            g4[:].rearrange("p t (c i) -> p c t i", i=4),
        )
        w_grouped0 = keep.tile([P, 1, N, PACK], BF16, name="w_grouped0", align_bytes=64)
        w_codes0 = keep.tile([P, N], U32, name="w_codes0", align_bytes=64)
        w_scales0 = keep.tile([P, N], U8, name="w_scales0", align_bytes=64)
        interleave_weights((nc.vector.tensor_copy,), 0, w_grouped0)
        quantize(w_codes0[:], w_scales0[:], w_grouped0[:].rearrange("p e n j -> p (e n j)"))

        codes0 = keep.tile([P, C], U32, name="codes0", align_bytes=64)
        scales0 = keep.tile([P, C], U8, name="scales0", align_bytes=64)
        quantize(codes0[:], scales0[:], grouped0[:])
        acc0 = multiply("acc0", C, w_codes0, w_scales0, 0, codes0[:], scales0[:])
        w_grouped1 = keep.tile([P, 1, N, PACK], BF16, name="w_grouped1", tag="after_qw01", align_bytes=64)
        w_codes1 = keep.tile([P, N], U32, name="w_codes1", align_bytes=64)
        w_scales1 = keep.tile([P, N], U8, name="w_scales1", align_bytes=64)
        nc.vector.tensor_copy(
            w_grouped1[:, 0, :, :].rearrange("p (c i) j -> p c j i", i=4),
            w_rows[1].rearrange("p j (c i) -> p c j i", i=4),
        )
        quantize(w_codes1[:], w_scales1[:], w_grouped1[:].rearrange("p e n j -> p (e n j)"))
        codes1 = keep.tile([P, C], U32, name="codes1", tag="after_qw01", align_bytes=64)
        scales1 = keep.tile([P, C], U8, name="scales1", align_bytes=64)
        quantize(codes1[:], scales1[:], grouped1[:])
        acc1 = multiply("acc1", C, w_codes1, w_scales1, 0, codes1[:], scales1[:])
        codes3a = keep.tile([P, H], U32, name="codes3a", tag="after_q1", align_bytes=64)
        scales3a = keep.tile([P, H], U8, name="scales3a", align_bytes=64)
        quantize(codes3a[:], scales3a[:], grouped3a[:])

        w_grouped23 = keep.tile([P, 2, N, PACK], BF16, name="w_grouped23", align_bytes=64)
        interleave_weights((nc.vector.tensor_copy, nc.scalar.copy), 1, w_grouped23)
        late = keep.tile([P, (C + H) * PACK], BF16, name="grouped_late", tag="after_w3", align_bytes=64)
        grouped2 = late[:, 0 : C * PACK]
        grouped3b = late[:, C * PACK : (C + H) * PACK]
        sums0 = keep.tile([P, C], F32, name="sums0", tag="after_sc0", align_bytes=64)
        nc.vector.tensor_copy(sums0[:], acc0[:])
        scalar_gather(grouped2, 0, 2 * C, C)
        sums1 = keep.tile([P, C], F32, name="sums1", tag="after_sc1", align_bytes=64)
        nc.scalar.copy(sums1[:], acc1[:])
        for t in range(1, PACK):
            scalar_gather(grouped2, t, 2 * C, C)

        w_codes23 = keep.tile([P, 2 * N], U32, name="w_codes23", align_bytes=64)
        w_scales23 = keep.tile([P, 2 * N], U8, name="w_scales23", align_bytes=64)
        quantize(w_codes23[:], w_scales23[:], w_grouped23[:].rearrange("p e n j -> p (e n j)"))
        acc3a = multiply("acc3a", H, w_codes23, w_scales23, 1, codes3a[:], scales3a[:])
        put_back(sums0[:], 0, C)
        sums3a = keep.tile([P, H], F32, name="sums3a")
        nc.scalar.copy(sums3a[:], acc3a[:])
        for t in range(PACK):
            scalar_gather(grouped3b, t, 3 * C + H, H)
        put_back(sums1[:], C, C)

        codes2 = keep.tile([P, C], U32, name="codes2", tag="after_sc0", align_bytes=64)
        scales2 = keep.tile([P, C], U8, name="scales2", align_bytes=64)
        quantize(codes2[:], scales2[:], grouped2)
        acc2 = multiply("acc2", C, w_codes23, w_scales23, 0, codes2[:], scales2[:])
        put_back(sums3a[:], 3 * C, H)
        codes3b = keep.tile([P, H], U32, name="codes3b", tag="after_sc1", align_bytes=64)
        scales3b = keep.tile([P, H], U8, name="scales3b", align_bytes=64)
        quantize(codes3b[:], scales3b[:], grouped3b)
        acc3b = multiply("acc3b", H, w_codes23, w_scales23, 1, codes3b[:], scales3b[:])
        sums2 = keep.tile([P, C], F32, name="sums2")
        nc.scalar.copy(sums2[:], acc2[:])
        put_back(sums2[:], 2 * C, C)
        sums3b = keep.tile([P, H], F32, name="sums3b")
        nc.scalar.copy(sums3b[:], acc3b[:])
        put_back(sums3b[:], 3 * C + H, H)

        nc.sync.dma_start(out, window[:])
